import numpy as np
import ml_dtypes


def mxq(x, axis, fmt="e4m3"):
    dtype, down = {"e4m3": (ml_dtypes.float8_e4m3fn, 7), "e5m2": (ml_dtypes.float8_e5m2, 14)}[fmt]
    v = np.moveaxis(np.asarray(x, np.float32).astype(ml_dtypes.bfloat16).astype(np.float64), axis, -1)
    blocks = v.reshape(v.shape[:-1] + (-1, 32))
    amax = np.abs(blocks).max(-1, keepdims=True)
    byte = np.maximum(np.where(amax > 0, np.frexp(amax)[1] - 1 + 127, 0) - down, 1)
    scale = np.exp2(byte - 127.0)
    codes = (blocks / scale).astype(np.float32).astype(dtype).astype(np.float64)
    return np.moveaxis((codes * scale).reshape(v.shape), -1, axis)


WIDE = False


def mx_kscale(k):
    if not WIDE:
        return np.ones(k)
    levels = np.array([10, -10, 5, -5, 0])
    if k % 512:
        return np.exp2(np.random.permutation(np.resize(levels, k // 32))).repeat(32)
    a = np.empty((k // 512, 16))
    for p in range(k // 512):
        a[p, :8] = np.random.permutation(np.resize(levels, 8))
        for g in range(8):
            far = levels[np.abs(levels - a[p, g]) >= 10]
            a[p, g + 8] = far[np.random.randint(len(far))]
    return np.exp2(a.ravel()).repeat(32)


def f64(x):
    return np.asarray(x).astype(np.float64)


def striped(idx):
    return np.tile(np.asarray(idx).reshape(-1, 16).T, (8, 1)).astype(np.uint16)


def unstriped(offs):
    return offs[:16].T.reshape(-1).astype(np.int64)


def striped8(idx):
    return np.asarray(idx).reshape(8, -1, 16).transpose(0, 2, 1).reshape(128, -1).astype(np.uint16)


def unstriped8(offs):
    return offs.reshape(8, 16, -1).transpose(0, 2, 1).reshape(8, -1).astype(np.int64)


def pick8(x, idx, run):
    r = np.arange(len(x))
    return x[r[:, None], idx[r % (8 * run) // run]]


E2M1 = np.array([0.0, 0.5, 1.0, 1.5, 2.0, 3.0, 4.0, 6.0, -0.0, -0.5, -1.0, -1.5, -2.0, -3.0, -4.0, -6.0])


def pack_weight(w, fmt):
    k, n = w.shape
    w = f64(np.asarray(w, np.float32).astype(ml_dtypes.bfloat16)).reshape(k // 32, 32, n)
    amax = np.abs(w).max(1)
    if fmt == "e4m3":
        byte = np.frexp(amax)[1] - 1 + 127 - 7
    else:
        mant, ex = np.frexp(amax / 6.0)
        byte = np.where(mant > 0.5, ex, ex - 1) + 127
    byte = np.clip(np.where(amax > 0, byte, 1), 1, 254)
    scaled = (w * np.exp2(127.0 - byte)[:, None, :]).reshape(k, n).astype(np.float32)
    by_word = np.ascontiguousarray(scaled.reshape(k // 512, 128, 4, n).transpose(0, 1, 3, 2))
    if fmt == "e4m3":
        words = by_word.astype(ml_dtypes.float8_e4m3fn).view(np.uint8)
    else:
        c = by_word.astype(ml_dtypes.float4_e2m1fn).view(np.uint8) & 0xF
        words = (c[..., 0::2] | (c[..., 1::2] << 4)).reshape(k // 512, 128, 2 * n)
    return np.ascontiguousarray(words), np.ascontiguousarray(byte.astype(np.uint8).reshape(k // 512, 16, n))


def unpack_weight(words, scales, fmt):
    g, _, n = scales.shape
    words = np.ascontiguousarray(words).reshape(g, 128, n, -1)
    if fmt == "e4m3":
        vals = words.view(ml_dtypes.float8_e4m3fn).astype(np.float64)
    else:
        nib = np.empty((g, 128, n, 4), np.uint8)
        nib[..., 0::2] = words & 0xF
        nib[..., 1::2] = words >> 4
        vals = E2M1[nib]
    vals = vals * np.repeat(np.exp2(scales.astype(np.float64) - 127.0), 8, axis=1)[..., None]
    return vals.transpose(0, 1, 3, 2).reshape(g * 512, n)


K, J, R, T, S, N, Z, U, E = 512, 512, 512, 1024, 256, 256, 1024, 1024, 256


def setup_inputs():
    n = np.random.standard_normal
    idx = np.random.permutation(T)[:J]
    idx2 = np.stack([np.random.permutation(J)[:S] for _ in range(8)])
    idx3 = np.stack([np.random.permutation(J)[:S] for _ in range(8)])
    idx4 = np.random.permutation(Z)[:N]
    idx5 = np.stack([np.random.permutation(U)[:J] for _ in range(8)])
    fk = mx_kscale(K)
    fr = mx_kscale(R)
    xtp = pack_weight(n((K, T)) * fk[:, None], "e2m1")
    wp = pack_weight(n((K, R)) * 1 / np.sqrt(K) / fk[:, None] * fr, "e4m3")
    w2p = pack_weight(n((K, R)) * 1 / np.sqrt(K) / fk[:, None] * fr, "e4m3")
    vsp = pack_weight(n((R, Z)) * 1 / np.sqrt(R) / fr[:, None], "e4m3")
    return {
        "xt_words": xtp[0],
        "xt_scales": xtp[1],
        "w_words": wp[0],
        "w_scales": wp[1],
        "w2_words": w2p[0],
        "w2_scales": w2p[1],
        "sa": (np.random.uniform(0.5, 1.6, (R, 1))).astype(np.float32),
        "vs_words": vsp[0],
        "vs_scales": vsp[1],
        "offs": striped(idx),
        "offs2": striped8(idx2),
        "offs3": striped8(idx3),
        "offs4": striped(idx4),
        "offs5": striped8(idx5),
    }


def reference(xt_words, xt_scales, w_words, w_scales, w2_words, w2_scales, sa, vs_words, vs_scales, offs, offs2, offs3, offs4, offs5):
    idx = unstriped(offs)
    idx2 = unstriped8(offs2)
    idx3 = unstriped8(offs3)
    idx4 = unstriped(offs4)
    idx5 = unstriped8(offs5)
    xtu = unpack_weight(xt_words, xt_scales, "e2m1")
    wu = unpack_weight(w_words, w_scales, "e4m3")
    w2u = unpack_weight(w2_words, w2_scales, "e4m3")
    vsu = unpack_weight(vs_words, vs_scales, "e4m3")
    xtidxg = xtu[:, idx]
    a = wu.T @ xtidxg
    b = w2u.T @ xtidxg
    h1 = pick8(a, idx2, 64) * f64(sa)
    pv = np.zeros((R, J))
    pv[np.arange(R)[:, None], idx3[np.arange(R) % 512 // 64]] = h1
    hid = np.abs(b - pv)
    vsidx4g = vsu[:, idx4]
    hidq = mxq(hid, 0, "e4m3")
    p = vsidx4g.T @ hidq
    m0 = np.zeros((N, U))
    m0[np.arange(N)[:, None], idx5[np.arange(N) % 128 // 16]] = p
    m1 = m0.reshape(N, E, U // E).mean(axis=2)
    m2 = np.repeat(m1, U // E, axis=1)
    y = m0 - m2
    return y

@@ -1,0 +1,232 @@
+from contextlib import ExitStack
+
+import concourse.mybir as mybir
+
+K, J, R, T, S, N, Z, U = 512, 512, 512, 1024, 256, 256, 1024, 1024
+FLOPS = 2 * K * R * J * 2 + 2 * R * N * J
+
+F32 = mybir.dt.float32
+BF16 = mybir.dt.bfloat16
+I32 = mybir.dt.int32
+U32 = mybir.dt.uint32
+U16 = mybir.dt.uint16
+U8 = mybir.dt.uint8
+FP8X4 = mybir.dt.float8_e4m3fn_x4
+FP4X4 = mybir.dt.float4_e2m1fn_x4
+ALU = mybir.AluOpType
+COPY = mybir.ActivationFunctionType.Copy
+ABS = mybir.ActivationFunctionType.Abs
+AXIS_X = mybir.AxisListType.X
+
+P = 128
+PACK = 4
+BUCKET = 4
+HEAD_PIECES = [256, 128, 128]
+SLOT_PIECES = [128, 128, 128, 128]
+PAGE_PIECES = [128, 128]
+
+
+def pieces(widths):
+    starts = [sum(widths[:i]) for i in range(len(widths))]
+    return [slice(s, s + w) for s, w in zip(starts, widths)]
+
+
+def entries(offsets, cols):
+    return offsets[:, cols.start // 16 : cols.stop // 16]
+
+
+def tile_picked_tokens_plain_twin_handover_store_endcontrast_kernel(
+    tc, xt_words, xt_scales, w_words, w_scales, w2_words, w2_scales, sa, vs_words, vs_scales,
+    offs, offs2, offs3, offs4, offs5, out,
+):
+    nc = tc.nc
+    with ExitStack() as ctx:
+        keep = ctx.enter_context(tc.tile_pool(name="keep", bufs=1))
+        banks = ctx.enter_context(tc.psum_pool(name="banks", bufs=4))
+
+        def sb(name, shape, dtype, tag=None):
+            return keep.tile(shape, dtype, name=name, tag=tag or name, align_bytes=64)
+
+        def load_list(name, src):
+            tile = sb(name, list(src.shape), U16)
+            nc.sync.dma_start(tile[:], src)
+            return tile
+
+        def load_words(name, src, width, dtype):
+            tile = sb(name, [P, width], dtype)
+            nc.sync.dma_start(tile[:].bitcast(I32), src.bitcast(I32))
+            return tile
+
+        def cleared_plane(name, width):
+            tile = sb(name, [P, width], U8)
+            nc.vector.memset(tile[:].bitcast(I32), 0)
+            return tile
+
+        def load_scale_rows(tile, src):
+            for q in range(4):
+                nc.sync.dma_start(tile[32 * q : 32 * q + 4, :].bitcast(I32), src[0, 4 * q : 4 * q + 4, :].bitcast(I32))
+
+        def flat(words):
+            return words[0].rearrange("p n t -> p (n t)")
+
+        def mx(acc, lhs, lhs_scale, rhs, rhs_scale):
+            nc.tensor.matmul_mx(out=acc, lhsT=lhs.bitcast(FP8X4), lhsT_scale=lhs_scale, rhs=rhs, rhs_scale=rhs_scale, start=True, stop=True)
+
+        x_s = cleared_plane("x_s", T)
+        w_s = cleared_plane("w_s", R)
+        w2_s = cleared_plane("w2_s", R)
+        v_s = cleared_plane("v_s", Z)
+
+        l_tok = load_list("l_tok", offs)
+        w_rows = sb("w_rows", [4, 4, R], U8)
+        nc.sync.dma_start(w_rows[:].bitcast(I32), w_scales[0].rearrange("(q i) n -> i q n", i=4).bitcast(I32))
+        x_w = load_words("x_w", xt_words[0], T, U16)
+        w_w = load_words("w_w", flat(w_words), R, U32)
+        load_scale_rows(x_s, xt_scales)
+        l_from = load_list("l_from", offs2)
+        sa_sb = sb("sa_sb", [P, PACK], F32)
+        nc.sync.dma_start(sa_sb[:], sa.rearrange("(p t) o -> p (t o)", t=PACK))
+        l_to = load_list("l_to", offs3)
+        w2_w = load_words("w2_w", flat(w2_words), R, U32)
+        load_scale_rows(w2_s, w2_scales)
+        l_store = load_list("l_store", offs4)
+        load_scale_rows(v_s, vs_scales)
+        v_w = load_words("v_w", flat(vs_words), Z, U32)
+        l_page = load_list("l_page", offs5)
+
+        pv = [sb("pv%d" % t, [P, J], F32) for t in range(1)]
+        for tile in pv:
+            nc.vector.memset(tile[:], 0.0)
+
+        wd_w = sb("wd_w", [P, PACK, P], U32)
+        wd_s = sb("wd_s", [P, PACK, P], U8)
+        for q in range(4):
+            nc.vector.tensor_copy(w_s[32 * q : 32 * q + 4, :].bitcast(I32), w_rows[:, q, :].bitcast(I32))
+        nc.scalar.copy(wd_w[:].rearrange("p t m -> p m t"), w_w[:].rearrange("p (m t) -> p m t", t=PACK))
+        w_s_dealt = w_s[:].rearrange("p (m t) -> p t m", t=PACK)
+        nc.vector.tensor_copy(wd_s[:, 0, :], w_s_dealt[:, 0, :])
+
+        xg_w = sb("xg_w", [P, J], U16)
+        xg_s = sb("xg_s", [P, J], U8)
+        nc.vector.tensor_copy(xg_w[:], x_w[:].indirect(l_tok[:]))
+        a_sb = [sb("a_sb%d" % t, [P, J], F32) for t in range(PACK)]
+        for cols in pieces(HEAD_PIECES):
+            nc.vector.tensor_copy(xg_s[:, cols], x_s[:].indirect(entries(l_tok, cols)))
+            acc = banks.tile([P, J], F32, name="acc", tag="acc")
+            mx(acc[:, cols], wd_w[:, 0, :], wd_s[:, 0, :], xg_w[:, cols].bitcast(FP4X4), xg_s[:, cols])
+            nc.scalar.copy(a_sb[0][:, cols], acc[:, cols])
+        nc.vector.tensor_copy(wd_s[:, 1:, :], w_s_dealt[:, 1:, :])
+        for t in range(1, PACK):
+            acc = banks.tile([P, J], F32, name="acc", tag="acc")
+            mx(acc[:], wd_w[:, t, :], wd_s[:, t, :], xg_w[:].bitcast(FP4X4), xg_s[:])
+            nc.vector.tensor_copy(a_sb[t][:], acc[:])
+
+        for t, tag in [(1, "wd_w"), (2, "wd_s"), (3, "x_s")]:
+            pv.append(sb("pv%d" % t, [P, J], F32, tag=tag))
+            nc.gpsimd.memset(pv[t][:], 0.0)
+
+        w2d_w = sb("w2d_w", [P, PACK, P], U32)
+        w2d_s = sb("w2d_s", [P, PACK, P], U8)
+        nc.vector.tensor_copy(w2d_w[:].rearrange("p t m -> p m t"), w2_w[:].rearrange("p (m t) -> p m t", t=PACK))
+        nc.vector.tensor_copy(w2d_s[:], w2_s[:].rearrange("p (m t) -> p t m", t=PACK))
+        b_ps = [banks.tile([P, J], F32, name="b_ps", tag="b_ps") for t in range(PACK)]
+        for t in range(PACK):
+            mx(b_ps[t][:], w2d_w[:, t, :], w2d_s[:, t, :], xg_w[:].bitcast(FP4X4), xg_s[:])
+
+        page = [sb("page%d" % i, [P, U], F32, tag=tag) for i, tag in enumerate(["w2_s", "w2_w"])]
+        for tile in page:
+            nc.gpsimd.memset(tile[:], 0.0)
+
+        vg_w = sb("vg_w", [P, N], U32)
+        vg_s = sb("vg_s", [P, N], U8)
+        nc.vector.tensor_copy(vg_s[:], v_s[:].indirect(l_store[:]))
+        nc.vector.tensor_copy(vg_w[:], v_w[:].indirect(l_store[:]))
+
+        h1 = [sb("h1_%d" % t, [P, S], F32) for t in range(PACK)]
+        diff = sb("diff", [P, 2, J], F32)
+        halves = sb("halves", [P, 2 * J, 2], BF16)
+        hid = sb("hid", [P, J, PACK], BF16)
+
+        def fetch(t):
+            nc.scalar.activation(out=h1[t][:], in_=a_sb[t][:].indirect(l_from[:]), func=COPY, scale=sa_sb[:, t : t + 1])
+
+        def hand_over(t):
+            nc.scalar.activation(out=pv[t][:].indirect(l_to[:]), in_=h1[t][:], func=COPY)
+
+        def subtract(t, cols):
+            nc.vector.tensor_tensor(diff[:, t % 2, cols], b_ps[t][:, cols], pv[t][:, cols], ALU.subtract)
+
+        def magnitude(dst, cols):
+            pair = diff[:, :, cols].rearrange("p t j -> p j t")
+            nc.vector.scalar_tensor_tensor(dst, pair, -1.0, pair, ALU.mult, ALU.max)
+
+        every = slice(0, J)
+        first = slice(0, SLOT_PIECES[0])
+        later = slice(SLOT_PIECES[0], J)
+        fetch(0)
+        hand_over(0)
+        fetch(1)
+        fetch(2)
+        subtract(0, every)
+        hand_over(1)
+        fetch(3)
+        subtract(1, every)
+        magnitude(hid[:, first, 0:2], first)
+        magnitude(halves[:, later, :], later)
+        hand_over(2)
+        subtract(2, every)
+        hand_over(3)
+
+        hq_w = sb("hq_w", [P, J], U32)
+        hq_s = sb("hq_s", [P, J], U8)
+        p_sb = [sb("p_sb%d" % i, [P, J], F32) for i in range(N // P)]
+        half_words = halves[:].rearrange("p j e -> p (j e)").bitcast(I32)
+        hid_words = hid[:].rearrange("p j t -> p (j t)").bitcast(I32).rearrange("p (j h) -> p j h", h=2)
+
+        def product(i, cols):
+            rows = slice(i * P, (i + 1) * P)
+            acc = banks.tile([P, J], F32, name="acc", tag="acc")
+            mx(acc[:, cols], vg_w[:, rows], vg_s[:, rows], hq_w[:, cols].bitcast(FP8X4), hq_s[:, cols])
+            return acc[:, cols]
+
+        def put_on_page(i, cols):
+            nc.scalar.activation(out=page[i][:].indirect(entries(l_page, cols)), in_=p_sb[i][:, cols], func=COPY)
+
+        slot_pieces = pieces(SLOT_PIECES)
+        for c, cols in enumerate(slot_pieces):
+            subtract(3, cols)
+            width = cols.stop - cols.start
+            if c == 0:
+                magnitude(hid[:, cols, 2:4], cols)
+            else:
+                magnitude(halves[:, J : J + width, :], cols)
+                nc.vector.tensor_copy(hid_words[:, cols, :], half_words[:, cols.start : 2 * J - cols.start].rearrange("p (h j) -> p j h", h=2)[:, :width, :])
+            nc.vector.quantize_mx(out=hq_w[:, cols].bitcast(FP8X4), scales=hq_s[:, cols], in_=hid[:, cols, :].rearrange("p j t -> p (j t)"))
+            if c == 0:
+                for i in range(N // P):
+                    nc.scalar.copy(p_sb[i][:, cols], product(i, cols))
+                for i in range(N // P):
+                    put_on_page(i, cols)
+            else:
+                nc.vector.tensor_copy(p_sb[0][:, cols], product(0, cols))
+                put_on_page(0, cols)
+        for cols in pieces([128, 128, 256])[1:]:
+            nc.vector.tensor_copy(p_sb[1][:, cols], product(1, cols))
+        put_on_page(1, slice(slot_pieces[0].stop, J))
+
+        for i in range(N // P):
+            pair_sums = sb("pair_sums%d" % i, [P, U // BUCKET, 2], F32, tag="sums%d" % i)
+            sums = sb("sums%d" % i, [P, U // BUCKET], F32, tag="sums%d" % (i + 1))
+            res = sb("res%d" % i, [P, U // BUCKET, BUCKET], F32)
+            by_bucket = page[i][:].rearrange("p (e f) -> p e f", f=BUCKET)
+            for es in pieces(PAGE_PIECES):
+                nc.vector.tensor_tensor(pair_sums[:, es, :], by_bucket[:, es, 0:2], by_bucket[:, es, 2:4], ALU.add)
+            for es in pieces(PAGE_PIECES):
+                nc.vector.tensor_tensor(sums[:, es], pair_sums[:, es, 0], pair_sums[:, es, 1], ALU.add)
+            for es in pieces([128, 80, 48]):
+                wide = sums[:, es].unsqueeze(2).to_broadcast([P, es.stop - es.start, BUCKET])
+                nc.vector.scalar_tensor_tensor(res[:, es, :], wide, -1.0 / BUCKET, by_bucket[:, es, :], ALU.mult, ALU.add)
+                nc.sync.dma_start(
+                    out[i * P : (i + 1) * P, es.start * BUCKET : es.stop * BUCKET],
+                    res[:, es, :].rearrange("p e f -> p (e f)"),
+                )

@@ -22,7 +22,7 @@ P = 128
 PACK = 4
 BUCKET = 4
 HEAD_PIECES = [256, 128, 128]
-SLOT_PIECES = [128, 128, 128, 128]
+SLOT_PIECES = [64, 128, 128, 128, 64]
 PAGE_PIECES = [128, 128]
 
 
@@ -77,10 +77,10 @@ def tile_picked_tokens_plain_twin_handover_store_endcontrast_kernel(
         w2_s = cleared_plane("w2_s", R)
         v_s = cleared_plane("v_s", Z)
 
-        l_tok = load_list("l_tok", offs)
         w_rows = sb("w_rows", [4, 4, R], U8)
         nc.sync.dma_start(w_rows[:].bitcast(I32), w_scales[0].rearrange("(q i) n -> i q n", i=4).bitcast(I32))
         x_w = load_words("x_w", xt_words[0], T, U16)
+        l_tok = load_list("l_tok", offs)
         w_w = load_words("w_w", flat(w_words), R, U32)
         load_scale_rows(x_s, xt_scales)
         l_from = load_list("l_from", offs2)
@@ -144,7 +144,6 @@ def tile_picked_tokens_plain_twin_handover_store_endcontrast_kernel(
 
         h1 = [sb("h1_%d" % t, [P, S], F32) for t in range(PACK)]
         diff = sb("diff", [P, 2, J], F32)
-        halves = sb("halves", [P, 2 * J, 2], BF16)
         hid = sb("hid", [P, J, PACK], BF16)
 
         def fetch(t):
@@ -156,13 +155,14 @@ def tile_picked_tokens_plain_twin_handover_store_endcontrast_kernel(
         def subtract(t, cols):
             nc.vector.tensor_tensor(diff[:, t % 2, cols], b_ps[t][:, cols], pv[t][:, cols], ALU.subtract)
 
-        def magnitude(dst, cols):
-            pair = diff[:, :, cols].rearrange("p t j -> p j t")
-            nc.vector.scalar_tensor_tensor(dst, pair, -1.0, pair, ALU.mult, ALU.max)
+        def both_planes(cols):
+            return diff[:, :, cols].rearrange("p t j -> p j t")
+
+        def magnitude(t, cols):
+            pair = both_planes(cols)
+            nc.vector.scalar_tensor_tensor(hid[:, cols, t : t + 2], pair, -1.0, pair, ALU.mult, ALU.max)
 
         every = slice(0, J)
-        first = slice(0, SLOT_PIECES[0])
-        later = slice(SLOT_PIECES[0], J)
         fetch(0)
         hand_over(0)
         fetch(1)
@@ -171,8 +171,7 @@ def tile_picked_tokens_plain_twin_handover_store_endcontrast_kernel(
         hand_over(1)
         fetch(3)
         subtract(1, every)
-        magnitude(hid[:, first, 0:2], first)
-        magnitude(halves[:, later, :], later)
+        magnitude(0, every)
         hand_over(2)
         subtract(2, every)
         hand_over(3)
@@ -180,38 +179,39 @@ def tile_picked_tokens_plain_twin_handover_store_endcontrast_kernel(
         hq_w = sb("hq_w", [P, J], U32)
         hq_s = sb("hq_s", [P, J], U8)
         p_sb = [sb("p_sb%d" % i, [P, J], F32) for i in range(N // P)]
-        half_words = halves[:].rearrange("p j e -> p (j e)").bitcast(I32)
-        hid_words = hid[:].rearrange("p j t -> p (j t)").bitcast(I32).rearrange("p (j h) -> p j h", h=2)
 
-        def product(i, cols):
+        def product(i, parts):
             rows = slice(i * P, (i + 1) * P)
             acc = banks.tile([P, J], F32, name="acc", tag="acc")
-            mx(acc[:, cols], vg_w[:, rows], vg_s[:, rows], hq_w[:, cols].bitcast(FP8X4), hq_s[:, cols])
-            return acc[:, cols]
+            for cols in parts:
+                mx(acc[:, cols], vg_w[:, rows], vg_s[:, rows], hq_w[:, cols].bitcast(FP8X4), hq_s[:, cols])
+            return acc
 
         def put_on_page(i, cols):
             nc.scalar.activation(out=page[i][:].indirect(entries(l_page, cols)), in_=p_sb[i][:, cols], func=COPY)
 
+        for cols in pieces([64, 256, 192]):
+            subtract(3, cols)
         slot_pieces = pieces(SLOT_PIECES)
         for c, cols in enumerate(slot_pieces):
-            subtract(3, cols)
-            width = cols.stop - cols.start
-            if c == 0:
-                magnitude(hid[:, cols, 2:4], cols)
+            if c < 3:
+                nc.scalar.activation(out=hid[:, cols, 2:4], in_=both_planes(cols), func=ABS)
             else:
-                magnitude(halves[:, J : J + width, :], cols)
-                nc.vector.tensor_copy(hid_words[:, cols, :], half_words[:, cols.start : 2 * J - cols.start].rearrange("p (h j) -> p j h", h=2)[:, :width, :])
+                magnitude(2, cols)
             nc.vector.quantize_mx(out=hq_w[:, cols].bitcast(FP8X4), scales=hq_s[:, cols], in_=hid[:, cols, :].rearrange("p j t -> p (j t)"))
             if c == 0:
                 for i in range(N // P):
-                    nc.scalar.copy(p_sb[i][:, cols], product(i, cols))
+                    nc.scalar.copy(p_sb[i][:, cols], product(i, [cols])[:, cols])
                 for i in range(N // P):
                     put_on_page(i, cols)
             else:
-                nc.vector.tensor_copy(p_sb[0][:, cols], product(0, cols))
-                put_on_page(0, cols)
-        for cols in pieces([128, 128, 256])[1:]:
-            nc.vector.tensor_copy(p_sb[1][:, cols], product(1, cols))
+                nc.vector.tensor_copy(p_sb[0][:, cols], product(0, [cols])[:, cols])
+                if c < 3:
+                    put_on_page(0, cols)
+        put_on_page(0, slice(slot_pieces[3].start, J))
+        for parts in [[slice(64, 192), slice(192, 448)], [slice(448, 512)]]:
+            cols = slice(parts[0].start, parts[-1].stop)
+            nc.vector.tensor_copy(p_sb[1][:, cols], product(1, parts)[:, cols])
         put_on_page(1, slice(slot_pieces[0].stop, J))
 
         for i in range(N // P):

@@ -121,19 +121,19 @@ def tile_picked_tokens_plain_twin_handover_store_endcontrast_kernel(
             mx(acc[:], wd_w[:, t, :], wd_s[:, t, :], xg_w[:].bitcast(FP4X4), xg_s[:])
             nc.vector.tensor_copy(a_sb[t][:], acc[:])
 
-        for t, tag in [(1, "wd_w"), (2, "wd_s"), (3, "x_s")]:
+        w2d_w = sb("w2d_w", [P, PACK, P], U32)
+        w2d_s = sb("w2d_s", [P, PACK, P], U8)
+        nc.gpsimd.tensor_copy(w2d_w[:].rearrange("p t m -> p m t"), w2_w[:].rearrange("p (m t) -> p m t", t=PACK))
+        nc.gpsimd.tensor_copy(w2d_s[:], w2_s[:].rearrange("p (m t) -> p t m", t=PACK))
+        for t, tag in [(1, "x_s"), (2, "wd_w"), (3, "wd_s")]:
             pv.append(sb("pv%d" % t, [P, J], F32, tag=tag))
             nc.gpsimd.memset(pv[t][:], 0.0)
 
-        w2d_w = sb("w2d_w", [P, PACK, P], U32)
-        w2d_s = sb("w2d_s", [P, PACK, P], U8)
-        nc.vector.tensor_copy(w2d_w[:].rearrange("p t m -> p m t"), w2_w[:].rearrange("p (m t) -> p m t", t=PACK))
-        nc.vector.tensor_copy(w2d_s[:], w2_s[:].rearrange("p (m t) -> p t m", t=PACK))
         b_ps = [banks.tile([P, J], F32, name="b_ps", tag="b_ps") for t in range(PACK)]
         for t in range(PACK):
             mx(b_ps[t][:], w2d_w[:, t, :], w2d_s[:, t, :], xg_w[:].bitcast(FP4X4), xg_s[:])
 
-        page = [sb("page%d" % i, [P, U], F32, tag=tag) for i, tag in enumerate(["w2_s", "w2_w"])]
+        page = [sb("page%d" % i, [P, U], F32, tag=tag) for i, tag in enumerate(["w2d_w", "w2d_s"])]
         for tile in page:
             nc.gpsimd.memset(tile[:], 0.0)
 
@@ -166,9 +166,9 @@ def tile_picked_tokens_plain_twin_handover_store_endcontrast_kernel(
         fetch(0)
         hand_over(0)
         fetch(1)
-        fetch(2)
         subtract(0, every)
         hand_over(1)
+        fetch(2)
         fetch(3)
         subtract(1, every)
         magnitude(0, every)

@@ -16,14 +16,19 @@ FP4X4 = mybir.dt.float4_e2m1fn_x4
 ALU = mybir.AluOpType
 COPY = mybir.ActivationFunctionType.Copy
 ABS = mybir.ActivationFunctionType.Abs
-AXIS_X = mybir.AxisListType.X
 
 P = 128
 PACK = 4
+QUADRANTS = 4
 BUCKET = 4
+PAGES = N // P
+
 HEAD_PIECES = [256, 128, 128]
 SLOT_PIECES = [64, 128, 128, 128, 64]
-PAGE_PIECES = [128, 128]
+LAST_DIFF_PIECES = [64, 256, 192]
+SCALAR_PIECES = 3
+SUM_PIECES = [128, 128]
+STORE_PIECES = [128, 80, 48]
 
 
 def pieces(widths):
@@ -31,8 +36,8 @@ def pieces(widths):
     return [slice(s, s + w) for s, w in zip(starts, widths)]
 
 
-def entries(offsets, cols):
-    return offsets[:, cols.start // 16 : cols.stop // 16]
+def entries(offsets, span):
+    return offsets[:, span.start // 16 : span.stop // 16]
 
 
 def tile_picked_tokens_plain_twin_handover_store_endcontrast_kernel(
@@ -57,27 +62,32 @@ def tile_picked_tokens_plain_twin_handover_store_endcontrast_kernel(
             nc.sync.dma_start(tile[:].bitcast(I32), src.bitcast(I32))
             return tile
 
-        def cleared_plane(name, width):
+        def cleared_scale_tile(name, width):
             tile = sb(name, [P, width], U8)
             nc.vector.memset(tile[:].bitcast(I32), 0)
             return tile
 
+        def live_rows(tile, q):
+            return tile[32 * q : 32 * q + 4, :].bitcast(I32)
+
         def load_scale_rows(tile, src):
-            for q in range(4):
-                nc.sync.dma_start(tile[32 * q : 32 * q + 4, :].bitcast(I32), src[0, 4 * q : 4 * q + 4, :].bitcast(I32))
+            for q in range(QUADRANTS):
+                nc.sync.dma_start(live_rows(tile, q), src[0, 4 * q : 4 * q + 4, :].bitcast(I32))
 
         def flat(words):
             return words[0].rearrange("p n t -> p (n t)")
 
         def mx(acc, lhs, lhs_scale, rhs, rhs_scale):
-            nc.tensor.matmul_mx(out=acc, lhsT=lhs.bitcast(FP8X4), lhsT_scale=lhs_scale, rhs=rhs, rhs_scale=rhs_scale, start=True, stop=True)
+            nc.tensor.matmul_mx(
+                out=acc, lhsT=lhs.bitcast(FP8X4), lhsT_scale=lhs_scale, rhs=rhs, rhs_scale=rhs_scale, start=True, stop=True
+            )
 
-        x_s = cleared_plane("x_s", T)
-        w_s = cleared_plane("w_s", R)
-        w2_s = cleared_plane("w2_s", R)
-        v_s = cleared_plane("v_s", Z)
+        x_s = cleared_scale_tile("x_s", T)
+        w_s = cleared_scale_tile("w_s", R)
+        w2_s = cleared_scale_tile("w2_s", R)
+        v_s = cleared_scale_tile("v_s", Z)
 
-        w_rows = sb("w_rows", [4, 4, R], U8)
+        w_rows = sb("w_rows", [4, QUADRANTS, R], U8)
         nc.sync.dma_start(w_rows[:].bitcast(I32), w_scales[0].rearrange("(q i) n -> i q n", i=4).bitcast(I32))
         x_w = load_words("x_w", xt_words[0], T, U16)
         l_tok = load_list("l_tok", offs)
@@ -94,41 +104,40 @@ def tile_picked_tokens_plain_twin_handover_store_endcontrast_kernel(
         v_w = load_words("v_w", flat(vs_words), Z, U32)
         l_page = load_list("l_page", offs5)
 
-        pv = [sb("pv%d" % t, [P, J], F32) for t in range(1)]
-        for tile in pv:
-            nc.vector.memset(tile[:], 0.0)
+        pv = [sb("pv0", [P, J], F32)]
+        nc.vector.memset(pv[0][:], 0.0)
 
         wd_w = sb("wd_w", [P, PACK, P], U32)
         wd_s = sb("wd_s", [P, PACK, P], U8)
-        for q in range(4):
-            nc.vector.tensor_copy(w_s[32 * q : 32 * q + 4, :].bitcast(I32), w_rows[:, q, :].bitcast(I32))
+        for q in range(QUADRANTS):
+            nc.vector.tensor_copy(live_rows(w_s, q), w_rows[:, q, :].bitcast(I32))
         nc.scalar.copy(wd_w[:].rearrange("p t m -> p m t"), w_w[:].rearrange("p (m t) -> p m t", t=PACK))
-        w_s_dealt = w_s[:].rearrange("p (m t) -> p t m", t=PACK)
-        nc.vector.tensor_copy(wd_s[:, 0, :], w_s_dealt[:, 0, :])
+        w_s_by_plane = w_s[:].rearrange("p (m t) -> p t m", t=PACK)
+        nc.vector.tensor_copy(wd_s[:, 0, :], w_s_by_plane[:, 0, :])
 
         xg_w = sb("xg_w", [P, J], U16)
         xg_s = sb("xg_s", [P, J], U8)
         nc.vector.tensor_copy(xg_w[:], x_w[:].indirect(l_tok[:]))
         a_sb = [sb("a_sb%d" % t, [P, J], F32) for t in range(PACK)]
-        for cols in pieces(HEAD_PIECES):
-            nc.vector.tensor_copy(xg_s[:, cols], x_s[:].indirect(entries(l_tok, cols)))
+        for slots in pieces(HEAD_PIECES):
+            nc.vector.tensor_copy(xg_s[:, slots], x_s[:].indirect(entries(l_tok, slots)))
             acc = banks.tile([P, J], F32, name="acc", tag="acc")
-            mx(acc[:, cols], wd_w[:, 0, :], wd_s[:, 0, :], xg_w[:, cols].bitcast(FP4X4), xg_s[:, cols])
-            nc.scalar.copy(a_sb[0][:, cols], acc[:, cols])
-        nc.vector.tensor_copy(wd_s[:, 1:, :], w_s_dealt[:, 1:, :])
+            mx(acc[:, slots], wd_w[:, 0, :], wd_s[:, 0, :], xg_w[:, slots].bitcast(FP4X4), xg_s[:, slots])
+            nc.scalar.copy(a_sb[0][:, slots], acc[:, slots])
+        nc.vector.tensor_copy(wd_s[:, 1:, :], w_s_by_plane[:, 1:, :])
         for t in range(1, PACK):
             acc = banks.tile([P, J], F32, name="acc", tag="acc")
             mx(acc[:], wd_w[:, t, :], wd_s[:, t, :], xg_w[:].bitcast(FP4X4), xg_s[:])
             nc.vector.tensor_copy(a_sb[t][:], acc[:])
 
-        w2d_w = sb("w2d_w", [P, PACK, P], U32)
-        w2d_s = sb("w2d_s", [P, PACK, P], U8)
-        nc.gpsimd.tensor_copy(w2d_w[:].rearrange("p t m -> p m t"), w2_w[:].rearrange("p (m t) -> p m t", t=PACK))
-        nc.gpsimd.tensor_copy(w2d_s[:], w2_s[:].rearrange("p (m t) -> p t m", t=PACK))
         for t, tag in [(1, "x_s"), (2, "wd_w"), (3, "wd_s")]:
             pv.append(sb("pv%d" % t, [P, J], F32, tag=tag))
             nc.gpsimd.memset(pv[t][:], 0.0)
 
+        w2d_w = sb("w2d_w", [P, PACK, P], U32)
+        w2d_s = sb("w2d_s", [P, PACK, P], U8)
+        nc.vector.tensor_copy(w2d_w[:].rearrange("p t m -> p m t"), w2_w[:].rearrange("p (m t) -> p m t", t=PACK))
+        nc.vector.tensor_copy(w2d_s[:], w2_s[:].rearrange("p (m t) -> p t m", t=PACK))
         b_ps = [banks.tile([P, J], F32, name="b_ps", tag="b_ps") for t in range(PACK)]
         for t in range(PACK):
             mx(b_ps[t][:], w2d_w[:, t, :], w2d_s[:, t, :], xg_w[:].bitcast(FP4X4), xg_s[:])
@@ -146,86 +155,93 @@ def tile_picked_tokens_plain_twin_handover_store_endcontrast_kernel(
         diff = sb("diff", [P, 2, J], F32)
         hid = sb("hid", [P, J, PACK], BF16)
 
-        def fetch(t):
-            nc.scalar.activation(out=h1[t][:], in_=a_sb[t][:].indirect(l_from[:]), func=COPY, scale=sa_sb[:, t : t + 1])
+        def fetch(t, parcels=slice(0, S)):
+            window = a_sb[t][:].indirect(entries(l_from, parcels))
+            nc.scalar.activation(out=h1[t][:, parcels], in_=window, func=COPY, scale=sa_sb[:, t : t + 1])
 
-        def hand_over(t):
-            nc.scalar.activation(out=pv[t][:].indirect(l_to[:]), in_=h1[t][:], func=COPY)
+        def hand_over(t, parcels=slice(0, S)):
+            nc.scalar.activation(out=pv[t][:].indirect(entries(l_to, parcels)), in_=h1[t][:, parcels], func=COPY)
 
-        def subtract(t, cols):
-            nc.vector.tensor_tensor(diff[:, t % 2, cols], b_ps[t][:, cols], pv[t][:, cols], ALU.subtract)
+        def subtract(t, slots):
+            nc.vector.tensor_tensor(diff[:, t % 2, slots], b_ps[t][:, slots], pv[t][:, slots], ALU.subtract)
 
-        def both_planes(cols):
-            return diff[:, :, cols].rearrange("p t j -> p j t")
+        def both_planes(slots):
+            return diff[:, :, slots].rearrange("p t j -> p j t")
 
-        def magnitude(t, cols):
-            pair = both_planes(cols)
-            nc.vector.scalar_tensor_tensor(hid[:, cols, t : t + 2], pair, -1.0, pair, ALU.mult, ALU.max)
+        def magnitude(t, slots):
+            pair = both_planes(slots)
+            nc.vector.scalar_tensor_tensor(hid[:, slots, t : t + 2], pair, -1.0, pair, ALU.mult, ALU.max)
 
-        every = slice(0, J)
-        fetch(0)
-        hand_over(0)
+        every_slot = slice(0, J)
+        low, high = pieces([S // 2, S // 2])
+        fetch(0, low)
+        fetch(0, high)
+        hand_over(0, low)
         fetch(1)
-        subtract(0, every)
+        hand_over(0, high)
+        subtract(0, every_slot)
         hand_over(1)
         fetch(2)
         fetch(3)
-        subtract(1, every)
-        magnitude(0, every)
+        subtract(1, every_slot)
+        magnitude(0, every_slot)
         hand_over(2)
-        subtract(2, every)
+        subtract(2, every_slot)
         hand_over(3)
 
         hq_w = sb("hq_w", [P, J], U32)
         hq_s = sb("hq_s", [P, J], U8)
-        p_sb = [sb("p_sb%d" % i, [P, J], F32) for i in range(N // P)]
+        p_sb = [sb("p_sb%d" % i, [P, J], F32) for i in range(PAGES)]
 
         def product(i, parts):
             rows = slice(i * P, (i + 1) * P)
             acc = banks.tile([P, J], F32, name="acc", tag="acc")
-            for cols in parts:
-                mx(acc[:, cols], vg_w[:, rows], vg_s[:, rows], hq_w[:, cols].bitcast(FP8X4), hq_s[:, cols])
+            for slots in parts:
+                mx(acc[:, slots], vg_w[:, rows], vg_s[:, rows], hq_w[:, slots].bitcast(FP8X4), hq_s[:, slots])
             return acc
 
-        def put_on_page(i, cols):
-            nc.scalar.activation(out=page[i][:].indirect(entries(l_page, cols)), in_=p_sb[i][:, cols], func=COPY)
+        def put_on_page(i, slots):
+            nc.scalar.activation(out=page[i][:].indirect(entries(l_page, slots)), in_=p_sb[i][:, slots], func=COPY)
 
-        for cols in pieces([64, 256, 192]):
-            subtract(3, cols)
+        for slots in pieces(LAST_DIFF_PIECES):
+            subtract(3, slots)
         slot_pieces = pieces(SLOT_PIECES)
-        for c, cols in enumerate(slot_pieces):
-            if c < 3:
-                nc.scalar.activation(out=hid[:, cols, 2:4], in_=both_planes(cols), func=ABS)
+        for c, slots in enumerate(slot_pieces):
+            if c < SCALAR_PIECES:
+                nc.scalar.activation(out=hid[:, slots, 2:4], in_=both_planes(slots), func=ABS)
             else:
-                magnitude(2, cols)
-            nc.vector.quantize_mx(out=hq_w[:, cols].bitcast(FP8X4), scales=hq_s[:, cols], in_=hid[:, cols, :].rearrange("p j t -> p (j t)"))
+                magnitude(2, slots)
+            nc.vector.quantize_mx(
+                out=hq_w[:, slots].bitcast(FP8X4), scales=hq_s[:, slots], in_=hid[:, slots, :].rearrange("p j t -> p (j t)")
+            )
             if c == 0:
-                for i in range(N // P):
-                    nc.scalar.copy(p_sb[i][:, cols], product(i, [cols])[:, cols])
-                for i in range(N // P):
-                    put_on_page(i, cols)
+                for i in range(PAGES):
+                    nc.scalar.copy(p_sb[i][:, slots], product(i, [slots])[:, slots])
+                for i in range(PAGES):
+                    put_on_page(i, slots)
             else:
-                nc.vector.tensor_copy(p_sb[0][:, cols], product(0, [cols])[:, cols])
-                if c < 3:
-                    put_on_page(0, cols)
-        put_on_page(0, slice(slot_pieces[3].start, J))
-        for parts in [[slice(64, 192), slice(192, 448)], [slice(448, 512)]]:
-            cols = slice(parts[0].start, parts[-1].stop)
-            nc.vector.tensor_copy(p_sb[1][:, cols], product(1, parts)[:, cols])
+                nc.vector.tensor_copy(p_sb[0][:, slots], product(0, [slots])[:, slots])
+                if c < SCALAR_PIECES:
+                    put_on_page(0, slots)
+        put_on_page(0, slice(slot_pieces[SCALAR_PIECES].start, J))
+        wide_pass = slice(slot_pieces[2].start, slot_pieces[3].stop)
+        for parts in [[slot_pieces[1], wide_pass], [slot_pieces[4]]]:
+            slots = slice(parts[0].start, parts[-1].stop)
+            nc.vector.tensor_copy(p_sb[1][:, slots], product(1, parts)[:, slots])
         put_on_page(1, slice(slot_pieces[0].stop, J))
 
-        for i in range(N // P):
+        for i in range(PAGES):
             pair_sums = sb("pair_sums%d" % i, [P, U // BUCKET, 2], F32, tag="sums%d" % i)
             sums = sb("sums%d" % i, [P, U // BUCKET], F32, tag="sums%d" % (i + 1))
             res = sb("res%d" % i, [P, U // BUCKET, BUCKET], F32)
             by_bucket = page[i][:].rearrange("p (e f) -> p e f", f=BUCKET)
-            for es in pieces(PAGE_PIECES):
+            for es in pieces(SUM_PIECES):
                 nc.vector.tensor_tensor(pair_sums[:, es, :], by_bucket[:, es, 0:2], by_bucket[:, es, 2:4], ALU.add)
-            for es in pieces(PAGE_PIECES):
+            for es in pieces(SUM_PIECES):
                 nc.vector.tensor_tensor(sums[:, es], pair_sums[:, es, 0], pair_sums[:, es, 1], ALU.add)
-            for es in pieces([128, 80, 48]):
-                wide = sums[:, es].unsqueeze(2).to_broadcast([P, es.stop - es.start, BUCKET])
-                nc.vector.scalar_tensor_tensor(res[:, es, :], wide, -1.0 / BUCKET, by_bucket[:, es, :], ALU.mult, ALU.add)
+            for es in pieces(STORE_PIECES):
+                spread = sums[:, es].unsqueeze(2).to_broadcast([P, es.stop - es.start, BUCKET])
+                nc.vector.scalar_tensor_tensor(res[:, es, :], spread, -1.0 / BUCKET, by_bucket[:, es, :], ALU.mult, ALU.add)
                 nc.sync.dma_start(
                     out[i * P : (i + 1) * P, es.start * BUCKET : es.stop * BUCKET],
                     res[:, es, :].rearrange("p e f -> p (e f)"),

from contextlib import ExitStack

import concourse.mybir as mybir

K, J, R, T, S, N, Z, U = 512, 512, 512, 1024, 256, 256, 1024, 1024
FLOPS = 2 * K * R * J * 2 + 2 * R * N * J

F32 = mybir.dt.float32
BF16 = mybir.dt.bfloat16
I32 = mybir.dt.int32
U32 = mybir.dt.uint32
U16 = mybir.dt.uint16
U8 = mybir.dt.uint8
FP8X4 = mybir.dt.float8_e4m3fn_x4
FP4X4 = mybir.dt.float4_e2m1fn_x4
ALU = mybir.AluOpType
COPY = mybir.ActivationFunctionType.Copy
ABS = mybir.ActivationFunctionType.Abs

P = 128
PACK = 4
QUADRANTS = 4
BUCKET = 4
PAGES = N // P

HEAD_PIECES = [256, 128, 128]
SLOT_PIECES = [64, 128, 128, 128, 64]
LAST_DIFF_PIECES = [64, 256, 192]
SCALAR_PIECES = 3
SUM_PIECES = [128, 128]
STORE_PIECES = [128, 80, 48]


def pieces(widths):
    starts = [sum(widths[:i]) for i in range(len(widths))]
    return [slice(s, s + w) for s, w in zip(starts, widths)]


def entries(offsets, span):
    return offsets[:, span.start // 16 : span.stop // 16]


def tile_picked_tokens_plain_twin_handover_store_endcontrast_kernel(
    tc, xt_words, xt_scales, w_words, w_scales, w2_words, w2_scales, sa, vs_words, vs_scales,
    offs, offs2, offs3, offs4, offs5, out,
):
    nc = tc.nc
    with ExitStack() as ctx:
        keep = ctx.enter_context(tc.tile_pool(name="keep", bufs=1))
        banks = ctx.enter_context(tc.psum_pool(name="banks", bufs=4))

        def sb(name, shape, dtype, tag=None):
            return keep.tile(shape, dtype, name=name, tag=tag or name, align_bytes=64)

        def load_list(name, src):
            tile = sb(name, list(src.shape), U16)
            nc.sync.dma_start(tile[:], src)
            return tile

        def load_words(name, src, width, dtype):
            tile = sb(name, [P, width], dtype)
            nc.sync.dma_start(tile[:].bitcast(I32), src.bitcast(I32))
            return tile

        def cleared_scale_tile(name, width):
            tile = sb(name, [P, width], U8)
            nc.vector.memset(tile[:].bitcast(I32), 0)
            return tile

        def live_rows(tile, q):
            return tile[32 * q : 32 * q + 4, :].bitcast(I32)

        def load_scale_rows(tile, src):
            for q in range(QUADRANTS):
                nc.sync.dma_start(live_rows(tile, q), src[0, 4 * q : 4 * q + 4, :].bitcast(I32))

        def flat(words):
            return words[0].rearrange("p n t -> p (n t)")

        def mx(acc, lhs, lhs_scale, rhs, rhs_scale):
            nc.tensor.matmul_mx(
                out=acc, lhsT=lhs.bitcast(FP8X4), lhsT_scale=lhs_scale, rhs=rhs, rhs_scale=rhs_scale, start=True, stop=True
            )

        x_s = cleared_scale_tile("x_s", T)
        w_s = cleared_scale_tile("w_s", R)
        w2_s = cleared_scale_tile("w2_s", R)
        v_s = cleared_scale_tile("v_s", Z)

        w_rows = sb("w_rows", [4, QUADRANTS, R], U8)
        nc.sync.dma_start(w_rows[:].bitcast(I32), w_scales[0].rearrange("(q i) n -> i q n", i=4).bitcast(I32))
        x_w = load_words("x_w", xt_words[0], T, U16)
        l_tok = load_list("l_tok", offs)
        w_w = load_words("w_w", flat(w_words), R, U32)
        load_scale_rows(x_s, xt_scales)
        l_from = load_list("l_from", offs2)
        sa_sb = sb("sa_sb", [P, PACK], F32)
        nc.sync.dma_start(sa_sb[:], sa.rearrange("(p t) o -> p (t o)", t=PACK))
        l_to = load_list("l_to", offs3)
        w2_w = load_words("w2_w", flat(w2_words), R, U32)
        load_scale_rows(w2_s, w2_scales)
        l_store = load_list("l_store", offs4)
        load_scale_rows(v_s, vs_scales)
        v_w = load_words("v_w", flat(vs_words), Z, U32)
        l_page = load_list("l_page", offs5)

        pv = [sb("pv0", [P, J], F32)]
        nc.vector.memset(pv[0][:], 0.0)

        wd_w = sb("wd_w", [P, PACK, P], U32)
        wd_s = sb("wd_s", [P, PACK, P], U8)
        for q in range(QUADRANTS):
            nc.vector.tensor_copy(live_rows(w_s, q), w_rows[:, q, :].bitcast(I32))
        nc.scalar.copy(wd_w[:].rearrange("p t m -> p m t"), w_w[:].rearrange("p (m t) -> p m t", t=PACK))
        w_s_by_plane = w_s[:].rearrange("p (m t) -> p t m", t=PACK)
        nc.vector.tensor_copy(wd_s[:, 0, :], w_s_by_plane[:, 0, :])

        xg_w = sb("xg_w", [P, J], U16)
        xg_s = sb("xg_s", [P, J], U8)
        nc.vector.tensor_copy(xg_w[:], x_w[:].indirect(l_tok[:]))
        a_sb = [sb("a_sb%d" % t, [P, J], F32) for t in range(PACK)]
        for slots in pieces(HEAD_PIECES):
            nc.vector.tensor_copy(xg_s[:, slots], x_s[:].indirect(entries(l_tok, slots)))
            acc = banks.tile([P, J], F32, name="acc", tag="acc")
            mx(acc[:, slots], wd_w[:, 0, :], wd_s[:, 0, :], xg_w[:, slots].bitcast(FP4X4), xg_s[:, slots])
            nc.scalar.copy(a_sb[0][:, slots], acc[:, slots])
        nc.vector.tensor_copy(wd_s[:, 1:, :], w_s_by_plane[:, 1:, :])
        for t in range(1, PACK):
            acc = banks.tile([P, J], F32, name="acc", tag="acc")
            mx(acc[:], wd_w[:, t, :], wd_s[:, t, :], xg_w[:].bitcast(FP4X4), xg_s[:])
            nc.vector.tensor_copy(a_sb[t][:], acc[:])

        for t, tag in [(1, "x_s"), (2, "wd_w"), (3, "wd_s")]:
            pv.append(sb("pv%d" % t, [P, J], F32, tag=tag))
            nc.gpsimd.memset(pv[t][:], 0.0)

        w2d_w = sb("w2d_w", [P, PACK, P], U32)
        w2d_s = sb("w2d_s", [P, PACK, P], U8)
        nc.vector.tensor_copy(w2d_w[:].rearrange("p t m -> p m t"), w2_w[:].rearrange("p (m t) -> p m t", t=PACK))
        nc.vector.tensor_copy(w2d_s[:], w2_s[:].rearrange("p (m t) -> p t m", t=PACK))
        b_ps = [banks.tile([P, J], F32, name="b_ps", tag="b_ps") for t in range(PACK)]
        for t in range(PACK):
            mx(b_ps[t][:], w2d_w[:, t, :], w2d_s[:, t, :], xg_w[:].bitcast(FP4X4), xg_s[:])

        page = [sb("page%d" % i, [P, U], F32, tag=tag) for i, tag in enumerate(["w2d_w", "w2d_s"])]
        for tile in page:
            nc.gpsimd.memset(tile[:], 0.0)

        vg_w = sb("vg_w", [P, N], U32)
        vg_s = sb("vg_s", [P, N], U8)
        nc.vector.tensor_copy(vg_s[:], v_s[:].indirect(l_store[:]))
        nc.vector.tensor_copy(vg_w[:], v_w[:].indirect(l_store[:]))

        h1 = [sb("h1_%d" % t, [P, S], F32) for t in range(PACK)]
        diff = sb("diff", [P, 2, J], F32)
        hid = sb("hid", [P, J, PACK], BF16)

        def fetch(t, parcels=slice(0, S)):
            window = a_sb[t][:].indirect(entries(l_from, parcels))
            nc.scalar.activation(out=h1[t][:, parcels], in_=window, func=COPY, scale=sa_sb[:, t : t + 1])

        def hand_over(t, parcels=slice(0, S)):
            nc.scalar.activation(out=pv[t][:].indirect(entries(l_to, parcels)), in_=h1[t][:, parcels], func=COPY)

        def subtract(t, slots):
            nc.vector.tensor_tensor(diff[:, t % 2, slots], b_ps[t][:, slots], pv[t][:, slots], ALU.subtract)

        def both_planes(slots):
            return diff[:, :, slots].rearrange("p t j -> p j t")

        def magnitude(t, slots):
            pair = both_planes(slots)
            nc.vector.scalar_tensor_tensor(hid[:, slots, t : t + 2], pair, -1.0, pair, ALU.mult, ALU.max)

        every_slot = slice(0, J)
        low, high = pieces([S // 2, S // 2])
        fetch(0, low)
        fetch(0, high)
        hand_over(0, low)
        fetch(1)
        hand_over(0, high)
        subtract(0, every_slot)
        hand_over(1)
        fetch(2)
        fetch(3)
        subtract(1, every_slot)
        magnitude(0, every_slot)
        hand_over(2)
        subtract(2, every_slot)
        hand_over(3)

        hq_w = sb("hq_w", [P, J], U32)
        hq_s = sb("hq_s", [P, J], U8)
        p_sb = [sb("p_sb%d" % i, [P, J], F32) for i in range(PAGES)]

        def product(i, parts):
            rows = slice(i * P, (i + 1) * P)
            acc = banks.tile([P, J], F32, name="acc", tag="acc")
            for slots in parts:
                mx(acc[:, slots], vg_w[:, rows], vg_s[:, rows], hq_w[:, slots].bitcast(FP8X4), hq_s[:, slots])
            return acc

        def put_on_page(i, slots):
            nc.scalar.activation(out=page[i][:].indirect(entries(l_page, slots)), in_=p_sb[i][:, slots], func=COPY)

        for slots in pieces(LAST_DIFF_PIECES):
            subtract(3, slots)
        slot_pieces = pieces(SLOT_PIECES)
        for c, slots in enumerate(slot_pieces):
            if c < SCALAR_PIECES:
                nc.scalar.activation(out=hid[:, slots, 2:4], in_=both_planes(slots), func=ABS)
            else:
                magnitude(2, slots)
            nc.vector.quantize_mx(
                out=hq_w[:, slots].bitcast(FP8X4), scales=hq_s[:, slots], in_=hid[:, slots, :].rearrange("p j t -> p (j t)")
            )
            if c == 0:
                for i in range(PAGES):
                    nc.scalar.copy(p_sb[i][:, slots], product(i, [slots])[:, slots])
                for i in range(PAGES):
                    put_on_page(i, slots)
            else:
                nc.vector.tensor_copy(p_sb[0][:, slots], product(0, [slots])[:, slots])
                if c < SCALAR_PIECES:
                    put_on_page(0, slots)
        put_on_page(0, slice(slot_pieces[SCALAR_PIECES].start, J))
        wide_pass = slice(slot_pieces[2].start, slot_pieces[3].stop)
        for parts in [[slot_pieces[1], wide_pass], [slot_pieces[4]]]:
            slots = slice(parts[0].start, parts[-1].stop)
            nc.vector.tensor_copy(p_sb[1][:, slots], product(1, parts)[:, slots])
        put_on_page(1, slice(slot_pieces[0].stop, J))

        for i in range(PAGES):
            pair_sums = sb("pair_sums%d" % i, [P, U // BUCKET, 2], F32, tag="sums%d" % i)
            sums = sb("sums%d" % i, [P, U // BUCKET], F32, tag="sums%d" % (i + 1))
            res = sb("res%d" % i, [P, U // BUCKET, BUCKET], F32)
            by_bucket = page[i][:].rearrange("p (e f) -> p e f", f=BUCKET)
            for es in pieces(SUM_PIECES):
                nc.vector.tensor_tensor(pair_sums[:, es, :], by_bucket[:, es, 0:2], by_bucket[:, es, 2:4], ALU.add)
            for es in pieces(SUM_PIECES):
                nc.vector.tensor_tensor(sums[:, es], pair_sums[:, es, 0], pair_sums[:, es, 1], ALU.add)
            for es in pieces(STORE_PIECES):
                spread = sums[:, es].unsqueeze(2).to_broadcast([P, es.stop - es.start, BUCKET])
                nc.vector.scalar_tensor_tensor(res[:, es, :], spread, -1.0 / BUCKET, by_bucket[:, es, :], ALU.mult, ALU.add)
                nc.sync.dma_start(
                    out[i * P : (i + 1) * P, es.start * BUCKET : es.stop * BUCKET],
                    res[:, es, :].rearrange("p e f -> p (e f)"),
                )
